import numpy as np
import ml_dtypes


def mxq(x, axis, fmt="e4m3"):
    dtype, down = {"e4m3": (ml_dtypes.float8_e4m3fn, 7), "e5m2": (ml_dtypes.float8_e5m2, 14)}[fmt]
    v = np.moveaxis(np.asarray(x, np.float32).astype(ml_dtypes.bfloat16).astype(np.float64), axis, -1)
    blocks = v.reshape(v.shape[:-1] + (-1, 32))
    amax = np.abs(blocks).max(-1, keepdims=True)
    byte = np.maximum(np.where(amax > 0, np.frexp(amax)[1] - 1 + 127, 0) - down, 1)
    scale = np.exp2(byte - 127.0)
    codes = (blocks / scale).astype(np.float32).astype(dtype).astype(np.float64)
    return np.moveaxis((codes * scale).reshape(v.shape), -1, axis)


WIDE = False


def mx_kscale(k):
    if not WIDE:
        return np.ones(k)
    levels = np.array([10, -10, 5, -5, 0])
    if k % 512:
        return np.exp2(np.random.permutation(np.resize(levels, k // 32))).repeat(32)
    a = np.empty((k // 512, 16))
    for p in range(k // 512):
        a[p, :8] = np.random.permutation(np.resize(levels, 8))
        for g in range(8):
            far = levels[np.abs(levels - a[p, g]) >= 10]
            a[p, g + 8] = far[np.random.randint(len(far))]
    return np.exp2(a.ravel()).repeat(32)


def f64(x):
    return np.asarray(x).astype(np.float64)


def striped(idx):
    return np.tile(np.asarray(idx).reshape(-1, 16).T, (8, 1)).astype(np.uint16)


def unstriped(offs):
    return offs[:16].T.reshape(-1).astype(np.int64)


B, N, T, D, DV, NQ = 1, 512, 2048, 512, 256, 512


def setup_inputs():
    n = np.random.standard_normal
    idx = np.sort(np.random.permutation(T)[:B * N].reshape(B, N), axis=1).reshape(-1)
    s = mx_kscale(D)[:, None]
    u = np.ones(T)
    u[idx] = mx_kscale(B * N)
    r = np.random.uniform(0.5, 2.0, T)
    qidx = np.random.permutation(T)[:B * NQ]
    k = n((D, T)) / s
    v = n((DV, T)) / (u * r)
    return {
        "xq": (n((D, T)) * s * (0.80 / np.sqrt(D))).astype(np.float32),
        "kT": k.astype(np.float32),
        "vT": v.astype(np.float32),
        "vs": np.tile(u * r, (128, 1)).astype(np.float32),
        "offs": striped(idx),
        "qoffs": striped(qidx),
    }


def reference(xq, kT, vT, vs, offs, qoffs):
    idx = unstriped(offs)
    k = f64(kT)
    v = f64(vT)
    pick = lambda x: x[:, idx].reshape(x.shape[0], B, N).transpose(1, 0, 2)
    q = f64(xq)[:, unstriped(qoffs)].reshape(D, B, NQ).transpose(1, 0, 2)
    score = mxq(q, 1, "e4m3").transpose(0, 2, 1) @ mxq(pick(k), 1, "e4m3")
    m = score.max(-1, keepdims=True)
    p = np.exp(score - m)
    total = p.sum(-1, keepdims=True)
    w = p * pick(f64(vs))[:, :1, :]
    y = mxq(w, 2, "e4m3") @ mxq(pick(v).transpose(0, 2, 1), 1, "e4m3")
    y = y / total
    out = np.zeros((DV, T))
    out[:, unstriped(qoffs)] = y.transpose(2, 0, 1).reshape(-1, B * NQ)
    return out

@@ -1,0 +1,220 @@
+from contextlib import ExitStack
+
+import concourse.mybir as mybir
+from concourse.masks import make_identity
+
+F32 = mybir.dt.float32
+BF16 = mybir.dt.bfloat16
+U32 = mybir.dt.uint32
+U16 = mybir.dt.uint16
+U8 = mybir.dt.uint8
+FP8X4 = mybir.dt.float8_e4m3fn_x4
+COPY = mybir.ActivationFunctionType.Copy
+EXP = mybir.ActivationFunctionType.Exp
+MULT = mybir.AluOpType.mult
+MAX = mybir.AluOpType.max
+AXIS_X = mybir.AxisListType.X
+
+P = 128
+PACK = 4
+T = 2048
+D = 512
+DV = 256
+N = 512
+NQ = 512
+Q_BLOCKS = NQ // P
+V_BLOCKS = DV // P
+HALVES = 2
+HALF_Q = NQ // HALVES
+
+FLOPS = 2 * NQ * N * D + 2 * NQ * N * DV
+BYTES = 4 * (2 * D * T + DV * T + T + DV * T) + 2 * 2 * P * (N // 16)
+
+
+def tile_attend_mod_sorted_kernel(tc, xq, kT, vT, vs, offs, qoffs, out):
+    nc = tc.nc
+    with ExitStack() as ctx:
+        keep = ctx.enter_context(tc.tile_pool(name="keep", bufs=1))
+        psum = ctx.enter_context(tc.psum_pool(name="psum", bufs=8))
+
+        q_list = keep.tile([P, NQ // 16], U16, name="q_list")
+        k_list = keep.tile([P, N // 16], U16, name="k_list")
+        nc.sync.dma_start(q_list[:], qoffs)
+        nc.sync.dma_start(k_list[:], offs)
+
+        vs_win = keep.tile([P, T], F32, name="vs_win")
+        nc.vector.memset(vs_win[:], 0.0)
+        warm = keep.tile([P, 1], F32, name="warm")
+        nc.vector.memset(warm[:], 0.0)
+        nc.scalar.activation(warm[:], warm[:], EXP)
+        out_wins = [keep.tile([P, T], F32, name="out_win%d" % e) for e in range(V_BLOCKS)]
+        for win in out_wins:
+            nc.gpsimd.memset(win[:], 0.0)
+        ident = keep.tile([P, P], F32, name="ident")
+        make_identity(nc, ident[:])
+
+        def load_planes(src, tag):
+            rows = src.rearrange("(p j) t -> p j t", j=PACK)
+            planes = []
+            for j in range(PACK):
+                plane = keep.tile([P, T], F32, name="%s_plane%d" % (tag, j))
+                nc.sync.dma_start(plane[:], rows[:, j, :])
+                planes.append(plane)
+                if tag == "q" and j == 0:
+                    nc.sync.dma_start(vs_win[0:1, :], vs[0:1, :])
+            return planes
+
+        q_planes = load_planes(xq, "q")
+        k_planes = load_planes(kT, "k")
+        v_planes = []
+        for e in range(V_BLOCKS):
+            plane = keep.tile([P, T], F32, name="v_plane%d" % e)
+            nc.sync.dma_start(plane[:], vT[e * P : (e + 1) * P, :])
+            v_planes.append(plane)
+
+        def quantize(grouped, width, tag):
+            codes = keep.tile([P, width], U32, align_bytes=64, name=tag + "_codes")
+            scales = keep.tile([P, width], U8, align_bytes=64, name=tag + "_scales")
+            nc.vector.quantize_mx(
+                out=codes[:].bitcast(FP8X4),
+                scales=scales[:],
+                in_=grouped[:].rearrange("p n j -> p (n j)"),
+            )
+            return codes, scales
+
+        def gather_planes(planes, offsets, count, tag):
+            grouped = keep.tile([P, count, PACK], BF16, align_bytes=64, name=tag + "_grouped")
+            for j in range(PACK):
+                nc.vector.tensor_copy(grouped[:, :, j], planes[j][:].indirect(offsets[:]))
+            return grouped
+
+        q_codes, q_scales = quantize(gather_planes(q_planes, q_list, NQ, "q"), NQ, "q")
+
+        vs_picked = keep.tile([P, N], F32, name="vs_picked")
+        nc.vector.tensor_copy(vs_picked[:], vs_win[:].indirect(k_list[:]))
+        vs_bank = psum.tile([P, PACK, P], F32, name="bank")
+        for t in range(PACK):
+            nc.tensor.transpose(vs_bank[:, t, :], vs_picked[:, t::PACK], ident[:])
+        vs_col = keep.tile([P, PACK], F32, name="vs_col")
+        nc.scalar.copy(vs_col[:], vs_bank[:, :, 0])
+
+        k_codes, k_scales = quantize(gather_planes(k_planes, k_list, N, "k"), N, "k")
+
+        neg_max = keep.tile([P, Q_BLOCKS], F32, name="neg_max")
+        total = keep.tile([P, Q_BLOCKS], F32, name="total")
+        inv_total = keep.tile([P, Q_BLOCKS], F32, name="inv_total")
+
+        w_codes = [keep.tile([P, HALF_Q], U32, align_bytes=64, name="w_codes%d" % h) for h in range(HALVES)]
+        w_scales = [keep.tile([P, HALF_Q], U8, align_bytes=64, name="w_scales%d" % h) for h in range(HALVES)]
+        v_grouped = keep.tile([P, DV, PACK], BF16, align_bytes=64, name="v_grouped")
+
+        score_banks = []
+        for b in range(Q_BLOCKS):
+            cols = slice(b * P, (b + 1) * P)
+            score = psum.tile([P, N], F32, name="bank")
+            nc.tensor.matmul_mx(
+                out=score[:],
+                lhsT=q_codes[:, cols].bitcast(FP8X4),
+                lhsT_scale=q_scales[:, cols],
+                rhs=k_codes[:].bitcast(FP8X4),
+                rhs_scale=k_scales[:],
+                start=True,
+                stop=True,
+            )
+            score_banks.append(score)
+
+        def value_block(e):
+            picked = keep.tile([P, N], F32, name="v_picked%d" % e)
+            nc.vector.tensor_copy(picked[:], v_planes[e][:].indirect(k_list[:]))
+            v_bank = psum.tile([P, PACK, P], F32, name="bank")
+            for t in range(PACK):
+                nc.tensor.transpose(v_bank[:, t, :], picked[:, t::PACK], ident[:])
+            nc.scalar.copy(v_grouped[:, e * P : (e + 1) * P, :], v_bank[:].rearrange("p t e -> p e t"))
+
+        def softmax(b):
+            score = score_banks[b]
+            nc.vector.tensor_reduce(neg_max[:, b : b + 1], score[:], AXIS_X, MAX, negate=True)
+            prob = keep.tile([P, PACK, P], F32, name="prob%d" % b)
+            nc.scalar.activation(
+                prob[:],
+                score[:].rearrange("p (s t) -> p t s", t=PACK),
+                EXP,
+                bias=neg_max[:, b : b + 1],
+                accum_out=total[:, b : b + 1],
+            )
+            turned = psum.tile([P, PACK, P], F32, name="bank")
+            for t in range(PACK):
+                nc.tensor.transpose(turned[:, t, :], prob[:, t, :], ident[:])
+            return turned
+
+        def weights(b, turned):
+            w = keep.tile([P, P, PACK], BF16, align_bytes=64, name="w%d" % b)
+            nc.vector.tensor_tensor(
+                w[:],
+                turned[:].rearrange("p t q -> p q t"),
+                vs_col[:].unsqueeze(1).to_broadcast([P, P, PACK]),
+                MULT,
+            )
+            h, i = divmod(b, Q_BLOCKS // HALVES)
+            cols = slice(i * P, (i + 1) * P)
+            nc.vector.quantize_mx(
+                out=w_codes[h][:, cols].bitcast(FP8X4),
+                scales=w_scales[h][:, cols],
+                in_=w[:].rearrange("p n j -> p (n j)"),
+            )
+
+        def products(h):
+            y_bank = psum.tile([P, V_BLOCKS, HALF_Q], F32, name="bank")
+            for e in range(V_BLOCKS):
+                cols = slice(e * P, (e + 1) * P)
+                nc.tensor.matmul_mx(
+                    out=y_bank[:, e, :],
+                    lhsT=v_codes[:, cols].bitcast(FP8X4),
+                    lhsT_scale=v_scales[:, cols],
+                    rhs=w_codes[h][:].bitcast(FP8X4),
+                    rhs_scale=w_scales[h][:],
+                    start=True,
+                    stop=True,
+                )
+            y = keep.tile([P, V_BLOCKS, HALF_Q], F32, name="y%d" % h)
+            nc.scalar.copy(y[:], y_bank[:])
+            return y
+
+        def divisors(h):
+            per_half = Q_BLOCKS // HALVES
+            blocks = slice(h * per_half, (h + 1) * per_half)
+            nc.vector.reciprocal(inv_total[:, blocks], total[:, blocks])
+            bank = psum.tile([P, HALF_Q], F32, name="bank")
+            for i in range(per_half):
+                b = h * per_half + i
+                nc.tensor.transpose(
+                    bank[:, i * P : (i + 1) * P], inv_total[:, b : b + 1].to_broadcast([P, P]), ident[:]
+                )
+            spread = keep.tile([P, HALF_Q], F32, name="spread%d" % h)
+            nc.scalar.copy(spread[:], bank[:])
+            return spread
+
+        def put_back(h, y, spread):
+            listed = q_list[:, h * HALF_Q // 16 : (h + 1) * HALF_Q // 16]
+            for e in range(V_BLOCKS):
+                nc.vector.tensor_tensor(out_wins[e][:].indirect(listed), y[:, e, :], spread[:], MULT)
+
+        value_block(0)
+        turned0 = softmax(0)
+        turned1 = softmax(1)
+        value_block(1)
+        turned2 = softmax(2)
+        weights(0, turned0)
+        turned3 = softmax(3)
+        weights(1, turned1)
+        v_codes, v_scales = quantize(v_grouped, DV, "v")
+        y0 = products(0)
+        spread0 = divisors(0)
+        weights(2, turned2)
+        weights(3, turned3)
+        y1 = products(1)
+        spread1 = divisors(1)
+        put_back(0, y0, spread0)
+        put_back(1, y1, spread1)
+        for e in range(V_BLOCKS):
+            nc.sync.dma_start(out[e * P : (e + 1) * P, :], out_wins[e][:])

@@ -39,19 +39,21 @@ def tile_attend_mod_sorted_kernel(tc, xq, kT, vT, vs, offs, qoffs, out):
 
         q_list = keep.tile([P, NQ // 16], U16, name="q_list")
         k_list = keep.tile([P, N // 16], U16, name="k_list")
-        nc.sync.dma_start(q_list[:], qoffs)
         nc.sync.dma_start(k_list[:], offs)
+        nc.sync.dma_start(q_list[:], qoffs)
 
         vs_win = keep.tile([P, T], F32, name="vs_win")
         nc.vector.memset(vs_win[:], 0.0)
         warm = keep.tile([P, 1], F32, name="warm")
         nc.vector.memset(warm[:], 0.0)
         nc.scalar.activation(warm[:], warm[:], EXP)
+        ident = keep.tile([P, P], F32, name="ident")
+        make_identity(nc, ident[:])
+        ident_bf16 = keep.tile([P, P], BF16, name="ident_bf16")
+        nc.scalar.copy(ident_bf16[:], ident[:])
         out_wins = [keep.tile([P, T], F32, name="out_win%d" % e) for e in range(V_BLOCKS)]
         for win in out_wins:
             nc.gpsimd.memset(win[:], 0.0)
-        ident = keep.tile([P, P], F32, name="ident")
-        make_identity(nc, ident[:])
 
         def load_planes(src, tag):
             rows = src.rearrange("(p j) t -> p j t", j=PACK)
@@ -60,12 +62,12 @@ def tile_attend_mod_sorted_kernel(tc, xq, kT, vT, vs, offs, qoffs, out):
                 plane = keep.tile([P, T], F32, name="%s_plane%d" % (tag, j))
                 nc.sync.dma_start(plane[:], rows[:, j, :])
                 planes.append(plane)
-                if tag == "q" and j == 0:
+                if tag == "k" and j == 0:
                     nc.sync.dma_start(vs_win[0:1, :], vs[0:1, :])
             return planes
 
-        q_planes = load_planes(xq, "q")
         k_planes = load_planes(kT, "k")
+        q_planes = load_planes(xq, "q")
         v_planes = []
         for e in range(V_BLOCKS):
             plane = keep.tile([P, T], F32, name="v_plane%d" % e)
@@ -78,17 +80,12 @@ def tile_attend_mod_sorted_kernel(tc, xq, kT, vT, vs, offs, qoffs, out):
             nc.vector.quantize_mx(
                 out=codes[:].bitcast(FP8X4),
                 scales=scales[:],
-                in_=grouped[:].rearrange("p n j -> p (n j)"),
+                in_=grouped.rearrange("p n j -> p (n j)"),
             )
             return codes, scales
 
-        def gather_planes(planes, offsets, count, tag):
-            grouped = keep.tile([P, count, PACK], BF16, align_bytes=64, name=tag + "_grouped")
-            for j in range(PACK):
-                nc.vector.tensor_copy(grouped[:, :, j], planes[j][:].indirect(offsets[:]))
-            return grouped
-
-        q_codes, q_scales = quantize(gather_planes(q_planes, q_list, NQ, "q"), NQ, "q")
+        k_grouped = keep.tile([P, N, PACK], BF16, align_bytes=64, name="k_grouped")
+        nc.vector.tensor_copy(k_grouped[:, :, 0], k_planes[0][:].indirect(k_list[:]))
 
         vs_picked = keep.tile([P, N], F32, name="vs_picked")
         nc.vector.tensor_copy(vs_picked[:], vs_win[:].indirect(k_list[:]))
@@ -97,42 +94,49 @@ def tile_attend_mod_sorted_kernel(tc, xq, kT, vT, vs, offs, qoffs, out):
             nc.tensor.transpose(vs_bank[:, t, :], vs_picked[:, t::PACK], ident[:])
         vs_col = keep.tile([P, PACK], F32, name="vs_col")
         nc.scalar.copy(vs_col[:], vs_bank[:, :, 0])
+        vs_row_bank = psum.tile([P, PACK, P], F32, name="bank")
+        for t in range(PACK):
+            nc.tensor.transpose(vs_row_bank[:, t, :], vs_col[:, t : t + 1].to_broadcast([P, P]), ident[:])
+        vs_row = keep.tile([P, PACK, P], F32, name="vs_row")
+        nc.scalar.copy(vs_row[:], vs_row_bank[:])
 
-        k_codes, k_scales = quantize(gather_planes(k_planes, k_list, N, "k"), N, "k")
+        for j in range(1, PACK):
+            nc.vector.tensor_copy(k_grouped[:, :, j], k_planes[j][:].indirect(k_list[:]))
+        k_codes, k_scales = quantize(k_grouped[:], N, "k")
+
+        q_grouped = keep.tile([P, NQ, PACK], BF16, align_bytes=64, name="q_grouped")
+        for j in range(PACK - 1):
+            nc.vector.tensor_copy(q_grouped[:, :, j], q_planes[j][:].indirect(q_list[:]))
 
         neg_max = keep.tile([P, Q_BLOCKS], F32, name="neg_max")
         total = keep.tile([P, Q_BLOCKS], F32, name="total")
         inv_total = keep.tile([P, Q_BLOCKS], F32, name="inv_total")
+        w_grouped = [keep.tile([P, HALF_Q, PACK], BF16, align_bytes=64, name="w_grouped%d" % h) for h in range(HALVES)]
+        lists = [q_list[:, h * HALF_Q // 16 : (h + 1) * HALF_Q // 16] for h in range(HALVES)]
 
-        w_codes = [keep.tile([P, HALF_Q], U32, align_bytes=64, name="w_codes%d" % h) for h in range(HALVES)]
-        w_scales = [keep.tile([P, HALF_Q], U8, align_bytes=64, name="w_scales%d" % h) for h in range(HALVES)]
-        v_grouped = keep.tile([P, DV, PACK], BF16, align_bytes=64, name="v_grouped")
+        def gather_last(h):
+            queries = slice(h * HALF_Q, (h + 1) * HALF_Q)
+            nc.vector.tensor_copy(q_grouped[:, queries, PACK - 1], q_planes[PACK - 1][:].indirect(lists[h]))
 
-        score_banks = []
-        for b in range(Q_BLOCKS):
-            cols = slice(b * P, (b + 1) * P)
+        def quantize_queries(h):
+            queries = slice(h * HALF_Q, (h + 1) * HALF_Q)
+            return quantize(q_grouped[:, queries, :], HALF_Q, "q%d" % h)
+
+        def scores(b, codes, scales):
+            cols = slice(b * P % HALF_Q, b * P % HALF_Q + P)
             score = psum.tile([P, N], F32, name="bank")
             nc.tensor.matmul_mx(
                 out=score[:],
-                lhsT=q_codes[:, cols].bitcast(FP8X4),
-                lhsT_scale=q_scales[:, cols],
+                lhsT=codes[:, cols].bitcast(FP8X4),
+                lhsT_scale=scales[:, cols],
                 rhs=k_codes[:].bitcast(FP8X4),
                 rhs_scale=k_scales[:],
                 start=True,
                 stop=True,
             )
-            score_banks.append(score)
+            return score
 
-        def value_block(e):
-            picked = keep.tile([P, N], F32, name="v_picked%d" % e)
-            nc.vector.tensor_copy(picked[:], v_planes[e][:].indirect(k_list[:]))
-            v_bank = psum.tile([P, PACK, P], F32, name="bank")
-            for t in range(PACK):
-                nc.tensor.transpose(v_bank[:, t, :], picked[:, t::PACK], ident[:])
-            nc.scalar.copy(v_grouped[:, e * P : (e + 1) * P, :], v_bank[:].rearrange("p t e -> p e t"))
-
-        def softmax(b):
-            score = score_banks[b]
+        def softmax(b, score):
             nc.vector.tensor_reduce(neg_max[:, b : b + 1], score[:], AXIS_X, MAX, negate=True)
             prob = keep.tile([P, PACK, P], F32, name="prob%d" % b)
             nc.scalar.activation(
@@ -142,79 +146,110 @@ def tile_attend_mod_sorted_kernel(tc, xq, kT, vT, vs, offs, qoffs, out):
                 bias=neg_max[:, b : b + 1],
                 accum_out=total[:, b : b + 1],
             )
+            return prob
+
+        def weights_gpsimd(b, prob):
+            flat = keep.tile([P, PACK, P], BF16, name="flat%d" % b)
+            nc.gpsimd.tensor_tensor(flat[:], prob[:], vs_row[:], MULT)
+            return flat
+
+        def turn_weights(b, flat):
+            h, i = divmod(b, Q_BLOCKS // HALVES)
+            turned = psum.tile([P, PACK, P], BF16, name="bank")
+            for t in range(PACK):
+                nc.tensor.transpose(turned[:, t, :], flat[:, t, :], ident_bf16[:])
+            nc.scalar.copy(w_grouped[h][:, i * P : (i + 1) * P, :], turned[:].rearrange("p t q -> p q t"))
+
+        def turn(prob):
             turned = psum.tile([P, PACK, P], F32, name="bank")
             for t in range(PACK):
                 nc.tensor.transpose(turned[:, t, :], prob[:, t, :], ident[:])
             return turned
 
-        def weights(b, turned):
-            w = keep.tile([P, P, PACK], BF16, align_bytes=64, name="w%d" % b)
+        def weights_vector(b, turned):
+            h, i = divmod(b, Q_BLOCKS // HALVES)
             nc.vector.tensor_tensor(
-                w[:],
+                w_grouped[h][:, i * P : (i + 1) * P, :],
                 turned[:].rearrange("p t q -> p q t"),
                 vs_col[:].unsqueeze(1).to_broadcast([P, P, PACK]),
                 MULT,
             )
-            h, i = divmod(b, Q_BLOCKS // HALVES)
-            cols = slice(i * P, (i + 1) * P)
-            nc.vector.quantize_mx(
-                out=w_codes[h][:, cols].bitcast(FP8X4),
-                scales=w_scales[h][:, cols],
-                in_=w[:].rearrange("p n j -> p (n j)"),
-            )
 
-        def products(h):
-            y_bank = psum.tile([P, V_BLOCKS, HALF_Q], F32, name="bank")
-            for e in range(V_BLOCKS):
-                cols = slice(e * P, (e + 1) * P)
-                nc.tensor.matmul_mx(
-                    out=y_bank[:, e, :],
-                    lhsT=v_codes[:, cols].bitcast(FP8X4),
-                    lhsT_scale=v_scales[:, cols],
-                    rhs=w_codes[h][:].bitcast(FP8X4),
-                    rhs_scale=w_scales[h][:],
-                    start=True,
-                    stop=True,
-                )
-            y = keep.tile([P, V_BLOCKS, HALF_Q], F32, name="y%d" % h)
-            nc.scalar.copy(y[:], y_bank[:])
+        def gather_values(e):
+            picked = keep.tile([P, N], F32, name="v_picked%d" % e)
+            nc.vector.tensor_copy(picked[:], v_planes[e][:].indirect(k_list[:]))
+            bank = psum.tile([P, PACK, P], F32, name="bank")
+            for t in range(PACK):
+                nc.tensor.transpose(bank[:, t, :], picked[:, t::PACK], ident[:])
+            grouped = keep.tile([P, P, PACK], BF16, align_bytes=64, name="v_grouped%d" % e)
+            nc.scalar.copy(grouped[:], bank[:].rearrange("p t e -> p e t"))
+            return grouped
+
+        def product(e, v, w):
+            bank = psum.tile([P, HALF_Q], F32, name="bank")
+            nc.tensor.matmul_mx(
+                out=bank[:],
+                lhsT=v[0][:].bitcast(FP8X4),
+                lhsT_scale=v[1][:],
+                rhs=w[0][:].bitcast(FP8X4),
+                rhs_scale=w[1][:],
+                start=True,
+                stop=True,
+            )
+            return bank
+
+        def to_sbuf(bank, name):
+            y = keep.tile([P, HALF_Q], F32, name=name)
+            nc.scalar.copy(y[:], bank[:])
             return y
 
-        def divisors(h):
-            per_half = Q_BLOCKS // HALVES
-            blocks = slice(h * per_half, (h + 1) * per_half)
-            nc.vector.reciprocal(inv_total[:, blocks], total[:, blocks])
-            bank = psum.tile([P, HALF_Q], F32, name="bank")
-            for i in range(per_half):
-                b = h * per_half + i
-                nc.tensor.transpose(
-                    bank[:, i * P : (i + 1) * P], inv_total[:, b : b + 1].to_broadcast([P, P]), ident[:]
-                )
-            spread = keep.tile([P, HALF_Q], F32, name="spread%d" % h)
-            nc.scalar.copy(spread[:], bank[:])
+        def divisors():
+            nc.vector.reciprocal(inv_total[:], total[:])
+            bank = psum.tile([P, Q_BLOCKS, P], F32, name="bank")
+            for b in range(Q_BLOCKS):
+                nc.tensor.transpose(bank[:, b, :], inv_total[:, b : b + 1].to_broadcast([P, P]), ident[:])
+            spread = keep.tile([P, NQ], F32, name="spread")
+            nc.scalar.copy(spread[:], bank[:].rearrange("p b q -> p (b q)"))
             return spread
 
-        def put_back(h, y, spread):
-            listed = q_list[:, h * HALF_Q // 16 : (h + 1) * HALF_Q // 16]
-            for e in range(V_BLOCKS):
-                nc.vector.tensor_tensor(out_wins[e][:].indirect(listed), y[:, e, :], spread[:], MULT)
+        def put_back(e, h, y, spread):
+            queries = slice(h * HALF_Q, (h + 1) * HALF_Q)
+            nc.vector.tensor_tensor(out_wins[e][:].indirect(lists[h]), y[:], spread[:, queries], MULT)
 
-        value_block(0)
-        turned0 = softmax(0)
-        turned1 = softmax(1)
-        value_block(1)
-        turned2 = softmax(2)
-        weights(0, turned0)
-        turned3 = softmax(3)
-        weights(1, turned1)
-        v_codes, v_scales = quantize(v_grouped, DV, "v")
-        y0 = products(0)
-        spread0 = divisors(0)
-        weights(2, turned2)
-        weights(3, turned3)
-        y1 = products(1)
-        spread1 = divisors(1)
-        put_back(0, y0, spread0)
-        put_back(1, y1, spread1)
-        for e in range(V_BLOCKS):
-            nc.sync.dma_start(out[e * P : (e + 1) * P, :], out_wins[e][:])
+        gather_last(0)
+        q0 = quantize_queries(0)
+        gather_last(1)
+        score0 = scores(0, *q0)
+        score1 = scores(1, *q0)
+        prob0 = softmax(0, score0)
+        flat0 = weights_gpsimd(0, prob0)
+        q1 = quantize_queries(1)
+        prob1 = softmax(1, score1)
+        flat1 = weights_gpsimd(1, prob1)
+        score2 = scores(2, *q1)
+        score3 = scores(3, *q1)
+        prob2 = softmax(2, score2)
+        prob3 = softmax(3, score3)
+        turned2 = turn(prob2)
+        v0_grouped = gather_values(0)
+        turn_weights(0, flat0)
+        turned3 = turn(prob3)
+        turn_weights(1, flat1)
+        v1_grouped = gather_values(1)
+        weights_vector(2, turned2)
+        v0 = quantize(v0_grouped[:], P, "v0")
+        w0 = quantize(w_grouped[0][:], HALF_Q, "w0")
+        y00 = to_sbuf(product(0, v0, w0), "y00")
+        weights_vector(3, turned3)
+        spread = divisors()
+        v1 = quantize(v1_grouped[:], P, "v1")
+        y01 = to_sbuf(product(1, v1, w0), "y01")
+        w1 = quantize(w_grouped[1][:], HALF_Q, "w1")
+        y10 = to_sbuf(product(0, v0, w1), "y10")
+        y11 = to_sbuf(product(1, v1, w1), "y11")
+        put_back(0, 0, y00, spread)
+        put_back(0, 1, y10, spread)
+        nc.sync.dma_start(out[0:P, :], out_wins[0][:])
+        put_back(1, 0, y01, spread)
+        put_back(1, 1, y11, spread)
+        nc.sync.dma_start(out[P:DV, :], out_wins[1][:])

@@ -178,6 +178,9 @@ def tile_attend_mod_sorted_kernel(tc, xq, kT, vT, vs, offs, qoffs, out):
         def gather_values(e):
             picked = keep.tile([P, N], F32, name="v_picked%d" % e)
             nc.vector.tensor_copy(picked[:], v_planes[e][:].indirect(k_list[:]))
+            return picked
+
+        def turn_values(e, picked):
             bank = psum.tile([P, PACK, P], F32, name="bank")
             for t in range(PACK):
                 nc.tensor.transpose(bank[:, t, :], picked[:, t::PACK], ident[:])
@@ -185,23 +188,21 @@ def tile_attend_mod_sorted_kernel(tc, xq, kT, vT, vs, offs, qoffs, out):
             nc.scalar.copy(grouped[:], bank[:].rearrange("p t e -> p e t"))
             return grouped
 
-        def product(e, v, w):
-            bank = psum.tile([P, HALF_Q], F32, name="bank")
-            nc.tensor.matmul_mx(
-                out=bank[:],
-                lhsT=v[0][:].bitcast(FP8X4),
-                lhsT_scale=v[1][:],
-                rhs=w[0][:].bitcast(FP8X4),
-                rhs_scale=w[1][:],
-                start=True,
-                stop=True,
-            )
-            return bank
-
-        def to_sbuf(bank, name):
-            y = keep.tile([P, HALF_Q], F32, name=name)
+        def products(blocks, w, name):
+            bank = psum.tile([P, len(blocks), HALF_Q], F32, name="bank")
+            for i, v in enumerate(blocks):
+                nc.tensor.matmul_mx(
+                    out=bank[:, i, :],
+                    lhsT=v[0][:].bitcast(FP8X4),
+                    lhsT_scale=v[1][:],
+                    rhs=w[0][:].bitcast(FP8X4),
+                    rhs_scale=w[1][:],
+                    start=True,
+                    stop=True,
+                )
+            y = keep.tile([P, len(blocks), HALF_Q], F32, name=name)
             nc.scalar.copy(y[:], bank[:])
-            return y
+            return [y[:, i, :] for i in range(len(blocks))]
 
         def divisors():
             nc.vector.reciprocal(inv_total[:], total[:])
@@ -214,7 +215,7 @@ def tile_attend_mod_sorted_kernel(tc, xq, kT, vT, vs, offs, qoffs, out):
 
         def put_back(e, h, y, spread):
             queries = slice(h * HALF_Q, (h + 1) * HALF_Q)
-            nc.vector.tensor_tensor(out_wins[e][:].indirect(lists[h]), y[:], spread[:, queries], MULT)
+            nc.vector.tensor_tensor(out_wins[e][:].indirect(lists[h]), y, spread[:, queries], MULT)
 
         gather_last(0)
         q0 = quantize_queries(0)
@@ -229,24 +230,25 @@ def tile_attend_mod_sorted_kernel(tc, xq, kT, vT, vs, offs, qoffs, out):
         score2 = scores(2, *q1)
         score3 = scores(3, *q1)
         prob2 = softmax(2, score2)
+        flat2 = weights_gpsimd(2, prob2)
         prob3 = softmax(3, score3)
-        turned2 = turn(prob2)
-        v0_grouped = gather_values(0)
         turn_weights(0, flat0)
+        picked0 = gather_values(0)
+        v0_grouped = turn_values(0, picked0)
         turned3 = turn(prob3)
         turn_weights(1, flat1)
-        v1_grouped = gather_values(1)
-        weights_vector(2, turned2)
+        picked1 = gather_values(1)
         v0 = quantize(v0_grouped[:], P, "v0")
         w0 = quantize(w_grouped[0][:], HALF_Q, "w0")
-        y00 = to_sbuf(product(0, v0, w0), "y00")
-        weights_vector(3, turned3)
         spread = divisors()
-        v1 = quantize(v1_grouped[:], P, "v1")
-        y01 = to_sbuf(product(1, v1, w0), "y01")
+        turn_weights(2, flat2)
+        weights_vector(3, turned3)
+        v1_grouped = turn_values(1, picked1)
+        (y00,) = products([v0], w0, "y00")
         w1 = quantize(w_grouped[1][:], HALF_Q, "w1")
-        y10 = to_sbuf(product(0, v0, w1), "y10")
-        y11 = to_sbuf(product(1, v1, w1), "y11")
+        v1 = quantize(v1_grouped[:], P, "v1")
+        y10, y11 = products([v0, v1], w1, "y1")
+        (y01,) = products([v1], w0, "y01")
         put_back(0, 0, y00, spread)
         put_back(0, 1, y10, spread)
         nc.sync.dma_start(out[0:P, :], out_wins[0][:])

@@ -9,7 +9,7 @@ U32 = mybir.dt.uint32
 U16 = mybir.dt.uint16
 U8 = mybir.dt.uint8
 FP8X4 = mybir.dt.float8_e4m3fn_x4
-COPY = mybir.ActivationFunctionType.Copy
+COPY_OUT = "p t x -> p x t"
 EXP = mybir.ActivationFunctionType.Exp
 MULT = mybir.AluOpType.mult
 MAX = mybir.AluOpType.max
@@ -22,162 +22,163 @@ D = 512
 DV = 256
 N = 512
 NQ = 512
-Q_BLOCKS = NQ // P
-V_BLOCKS = DV // P
+PER_LIST_COLUMN = 16
+Q_CHUNKS = NQ // P
+V_CHUNKS = DV // P
 HALVES = 2
 HALF_Q = NQ // HALVES
+PSUM_BANKS = 8
 
 FLOPS = 2 * NQ * N * D + 2 * NQ * N * DV
-BYTES = 4 * (2 * D * T + DV * T + T + DV * T) + 2 * 2 * P * (N // 16)
+BYTES = 4 * (2 * D * T + DV * T + T + DV * T) + 2 * P * (N + NQ) // PER_LIST_COLUMN
 
 
 def tile_attend_mod_sorted_kernel(tc, xq, kT, vT, vs, offs, qoffs, out):
     nc = tc.nc
     with ExitStack() as ctx:
         keep = ctx.enter_context(tc.tile_pool(name="keep", bufs=1))
-        psum = ctx.enter_context(tc.psum_pool(name="psum", bufs=8))
+        psum = ctx.enter_context(tc.psum_pool(name="psum", bufs=PSUM_BANKS))
 
-        q_list = keep.tile([P, NQ // 16], U16, name="q_list")
-        k_list = keep.tile([P, N // 16], U16, name="k_list")
+        k_list = keep.tile([P, N // PER_LIST_COLUMN], U16, name="k_list")
+        q_list = keep.tile([P, NQ // PER_LIST_COLUMN], U16, name="q_list")
         nc.sync.dma_start(k_list[:], offs)
         nc.sync.dma_start(q_list[:], qoffs)
 
-        vs_win = keep.tile([P, T], F32, name="vs_win")
-        nc.vector.memset(vs_win[:], 0.0)
-        warm = keep.tile([P, 1], F32, name="warm")
-        nc.vector.memset(warm[:], 0.0)
-        nc.scalar.activation(warm[:], warm[:], EXP)
+        vs_window = keep.tile([P, T], F32, name="vs_window")
+        nc.vector.memset(vs_window[:], 0.0)
+        table_column = keep.tile([P, 1], F32, name="table_column")
+        nc.vector.memset(table_column[:], 0.0)
+        nc.scalar.activation(table_column[:], table_column[:], EXP)
+
         ident = keep.tile([P, P], F32, name="ident")
         make_identity(nc, ident[:])
         ident_bf16 = keep.tile([P, P], BF16, name="ident_bf16")
         nc.scalar.copy(ident_bf16[:], ident[:])
-        out_wins = [keep.tile([P, T], F32, name="out_win%d" % e) for e in range(V_BLOCKS)]
-        for win in out_wins:
-            nc.gpsimd.memset(win[:], 0.0)
+        out_windows = [keep.tile([P, T], F32, name="out_window%d" % e) for e in range(V_CHUNKS)]
+        for window in out_windows:
+            nc.gpsimd.memset(window[:], 0.0)
 
-        def load_planes(src, tag):
-            rows = src.rearrange("(p j) t -> p j t", j=PACK)
-            planes = []
-            for j in range(PACK):
-                plane = keep.tile([P, T], F32, name="%s_plane%d" % (tag, j))
-                nc.sync.dma_start(plane[:], rows[:, j, :])
-                planes.append(plane)
-                if tag == "k" and j == 0:
-                    nc.sync.dma_start(vs_win[0:1, :], vs[0:1, :])
-            return planes
+        def load(rows, name):
+            tile = keep.tile([P, T], F32, name=name)
+            nc.sync.dma_start(tile[:], rows)
+            return tile
 
-        k_planes = load_planes(kT, "k")
-        q_planes = load_planes(xq, "q")
-        v_planes = []
-        for e in range(V_BLOCKS):
-            plane = keep.tile([P, T], F32, name="v_plane%d" % e)
-            nc.sync.dma_start(plane[:], vT[e * P : (e + 1) * P, :])
-            v_planes.append(plane)
+        k_rows = kT.rearrange("(p t) c -> p t c", t=PACK)
+        q_rows = xq.rearrange("(p t) c -> p t c", t=PACK)
+        k_tiles = [load(k_rows[:, 0, :], "k_tile0")]
+        nc.sync.dma_start(vs_window[0:1, :], vs[0:1, :])
+        k_tiles.extend([load(k_rows[:, t, :], "k_tile%d" % t) for t in range(1, PACK)])
+        q_tiles = [load(q_rows[:, t, :], "q_tile%d" % t) for t in range(PACK)]
+        v_tiles = [load(vT[e * P : (e + 1) * P, :], "v_tile%d" % e) for e in range(V_CHUNKS)]
 
-        def quantize(grouped, width, tag):
-            codes = keep.tile([P, width], U32, align_bytes=64, name=tag + "_codes")
-            scales = keep.tile([P, width], U8, align_bytes=64, name=tag + "_scales")
+        def quantize(grouped, width, name):
+            codes = keep.tile([P, width], U32, align_bytes=64, name=name + "_codes")
+            scales = keep.tile([P, width], U8, align_bytes=64, name=name + "_scales")
             nc.vector.quantize_mx(
                 out=codes[:].bitcast(FP8X4),
                 scales=scales[:],
-                in_=grouped.rearrange("p n j -> p (n j)"),
+                in_=grouped.rearrange("p c t -> p (c t)"),
             )
             return codes, scales
 
         k_grouped = keep.tile([P, N, PACK], BF16, align_bytes=64, name="k_grouped")
-        nc.vector.tensor_copy(k_grouped[:, :, 0], k_planes[0][:].indirect(k_list[:]))
+        nc.vector.tensor_copy(k_grouped[:, :, 0], k_tiles[0][:].indirect(k_list[:]))
 
         vs_picked = keep.tile([P, N], F32, name="vs_picked")
-        nc.vector.tensor_copy(vs_picked[:], vs_win[:].indirect(k_list[:]))
-        vs_bank = psum.tile([P, PACK, P], F32, name="bank")
+        nc.vector.tensor_copy(vs_picked[:], vs_window[:].indirect(k_list[:]))
+        column_bank = psum.tile([P, PACK, P], F32, name="bank")
         for t in range(PACK):
-            nc.tensor.transpose(vs_bank[:, t, :], vs_picked[:, t::PACK], ident[:])
-        vs_col = keep.tile([P, PACK], F32, name="vs_col")
-        nc.scalar.copy(vs_col[:], vs_bank[:, :, 0])
-        vs_row_bank = psum.tile([P, PACK, P], F32, name="bank")
+            nc.tensor.transpose(column_bank[:, t, :], vs_picked[:, t::PACK], ident[:])
+        vs_column = keep.tile([P, PACK], F32, name="vs_column")
+        nc.scalar.copy(vs_column[:], column_bank[:, :, 0])
+        row_bank = psum.tile([P, PACK, P], F32, name="bank")
         for t in range(PACK):
-            nc.tensor.transpose(vs_row_bank[:, t, :], vs_col[:, t : t + 1].to_broadcast([P, P]), ident[:])
+            nc.tensor.transpose(row_bank[:, t, :], vs_column[:, t : t + 1].to_broadcast([P, P]), ident[:])
         vs_row = keep.tile([P, PACK, P], F32, name="vs_row")
-        nc.scalar.copy(vs_row[:], vs_row_bank[:])
+        nc.scalar.copy(vs_row[:], row_bank[:])
 
-        for j in range(1, PACK):
-            nc.vector.tensor_copy(k_grouped[:, :, j], k_planes[j][:].indirect(k_list[:]))
+        for t in range(1, PACK):
+            nc.vector.tensor_copy(k_grouped[:, :, t], k_tiles[t][:].indirect(k_list[:]))
         k_codes, k_scales = quantize(k_grouped[:], N, "k")
 
         q_grouped = keep.tile([P, NQ, PACK], BF16, align_bytes=64, name="q_grouped")
-        for j in range(PACK - 1):
-            nc.vector.tensor_copy(q_grouped[:, :, j], q_planes[j][:].indirect(q_list[:]))
+        for t in range(PACK - 1):
+            nc.vector.tensor_copy(q_grouped[:, :, t], q_tiles[t][:].indirect(q_list[:]))
 
-        neg_max = keep.tile([P, Q_BLOCKS], F32, name="neg_max")
-        total = keep.tile([P, Q_BLOCKS], F32, name="total")
-        inv_total = keep.tile([P, Q_BLOCKS], F32, name="inv_total")
+        half_queries = [slice(h * HALF_Q, (h + 1) * HALF_Q) for h in range(HALVES)]
+        half_lists = [
+            q_list[:, h * HALF_Q // PER_LIST_COLUMN : (h + 1) * HALF_Q // PER_LIST_COLUMN] for h in range(HALVES)
+        ]
+        neg_max = keep.tile([P, Q_CHUNKS], F32, name="neg_max")
+        total = keep.tile([P, Q_CHUNKS], F32, name="total")
+        inv_total = keep.tile([P, Q_CHUNKS], F32, name="inv_total")
         w_grouped = [keep.tile([P, HALF_Q, PACK], BF16, align_bytes=64, name="w_grouped%d" % h) for h in range(HALVES)]
-        lists = [q_list[:, h * HALF_Q // 16 : (h + 1) * HALF_Q // 16] for h in range(HALVES)]
 
-        def gather_last(h):
-            queries = slice(h * HALF_Q, (h + 1) * HALF_Q)
-            nc.vector.tensor_copy(q_grouped[:, queries, PACK - 1], q_planes[PACK - 1][:].indirect(lists[h]))
+        def gather_last_queries(h):
+            last = PACK - 1
+            nc.vector.tensor_copy(q_grouped[:, half_queries[h], last], q_tiles[last][:].indirect(half_lists[h]))
 
         def quantize_queries(h):
-            queries = slice(h * HALF_Q, (h + 1) * HALF_Q)
-            return quantize(q_grouped[:, queries, :], HALF_Q, "q%d" % h)
+            return quantize(q_grouped[:, half_queries[h], :], HALF_Q, "q%d" % h)
 
         def scores(b, codes, scales):
-            cols = slice(b * P % HALF_Q, b * P % HALF_Q + P)
-            score = psum.tile([P, N], F32, name="bank")
+            start = b * P % HALF_Q
+            bank = psum.tile([P, N], F32, name="bank")
             nc.tensor.matmul_mx(
-                out=score[:],
-                lhsT=codes[:, cols].bitcast(FP8X4),
-                lhsT_scale=scales[:, cols],
+                out=bank[:],
+                lhsT=codes[:, start : start + P].bitcast(FP8X4),
+                lhsT_scale=scales[:, start : start + P],
                 rhs=k_codes[:].bitcast(FP8X4),
                 rhs_scale=k_scales[:],
                 start=True,
                 stop=True,
             )
-            return score
+            return bank
 
-        def softmax(b, score):
-            nc.vector.tensor_reduce(neg_max[:, b : b + 1], score[:], AXIS_X, MAX, negate=True)
+        def softmax(b, bank):
+            nc.vector.tensor_reduce(neg_max[:, b : b + 1], bank[:], AXIS_X, MAX, negate=True)
             prob = keep.tile([P, PACK, P], F32, name="prob%d" % b)
             nc.scalar.activation(
                 prob[:],
-                score[:].rearrange("p (s t) -> p t s", t=PACK),
+                bank[:].rearrange("p (s t) -> p t s", t=PACK),
                 EXP,
                 bias=neg_max[:, b : b + 1],
                 accum_out=total[:, b : b + 1],
             )
             return prob
 
-        def weights_gpsimd(b, prob):
-            flat = keep.tile([P, PACK, P], BF16, name="flat%d" % b)
-            nc.gpsimd.tensor_tensor(flat[:], prob[:], vs_row[:], MULT)
-            return flat
+        def w_columns(b):
+            h, i = divmod(b, Q_CHUNKS // HALVES)
+            return w_grouped[h][:, i * P : (i + 1) * P, :]
 
-        def turn_weights(b, flat):
-            h, i = divmod(b, Q_BLOCKS // HALVES)
-            turned = psum.tile([P, PACK, P], BF16, name="bank")
+        def multiply_on_gpsimd(b, prob):
+            weights = keep.tile([P, PACK, P], BF16, name="weights%d" % b)
+            nc.gpsimd.tensor_tensor(weights[:], prob[:], vs_row[:], MULT)
+            return weights
+
+        def turn_weights(b, weights):
+            bank = psum.tile([P, PACK, P], BF16, name="bank")
             for t in range(PACK):
-                nc.tensor.transpose(turned[:, t, :], flat[:, t, :], ident_bf16[:])
-            nc.scalar.copy(w_grouped[h][:, i * P : (i + 1) * P, :], turned[:].rearrange("p t q -> p q t"))
+                nc.tensor.transpose(bank[:, t, :], weights[:, t, :], ident_bf16[:])
+            nc.scalar.copy(w_columns(b), bank[:].rearrange(COPY_OUT))
 
-        def turn(prob):
-            turned = psum.tile([P, PACK, P], F32, name="bank")
+        def turn_probs(prob):
+            bank = psum.tile([P, PACK, P], F32, name="bank")
             for t in range(PACK):
-                nc.tensor.transpose(turned[:, t, :], prob[:, t, :], ident[:])
-            return turned
+                nc.tensor.transpose(bank[:, t, :], prob[:, t, :], ident[:])
+            return bank
 
-        def weights_vector(b, turned):
-            h, i = divmod(b, Q_BLOCKS // HALVES)
+        def multiply_on_vector(b, bank):
             nc.vector.tensor_tensor(
-                w_grouped[h][:, i * P : (i + 1) * P, :],
-                turned[:].rearrange("p t q -> p q t"),
-                vs_col[:].unsqueeze(1).to_broadcast([P, P, PACK]),
+                w_columns(b),
+                bank[:].rearrange(COPY_OUT),
+                vs_column[:].unsqueeze(1).to_broadcast([P, P, PACK]),
                 MULT,
             )
 
         def gather_values(e):
             picked = keep.tile([P, N], F32, name="v_picked%d" % e)
-            nc.vector.tensor_copy(picked[:], v_planes[e][:].indirect(k_list[:]))
+            nc.vector.tensor_copy(picked[:], v_tiles[e][:].indirect(k_list[:]))
             return picked
 
         def turn_values(e, picked):
@@ -185,73 +186,73 @@ def tile_attend_mod_sorted_kernel(tc, xq, kT, vT, vs, offs, qoffs, out):
             for t in range(PACK):
                 nc.tensor.transpose(bank[:, t, :], picked[:, t::PACK], ident[:])
             grouped = keep.tile([P, P, PACK], BF16, align_bytes=64, name="v_grouped%d" % e)
-            nc.scalar.copy(grouped[:], bank[:].rearrange("p t e -> p e t"))
+            nc.scalar.copy(grouped[:], bank[:].rearrange(COPY_OUT))
             return grouped
 
-        def products(blocks, w, name):
-            bank = psum.tile([P, len(blocks), HALF_Q], F32, name="bank")
-            for i, v in enumerate(blocks):
+        def products(values, halves, name):
+            v_codes, v_scales = values
+            bank = psum.tile([P, len(halves), HALF_Q], F32, name="bank")
+            for i, (w_codes, w_scales) in enumerate(halves):
                 nc.tensor.matmul_mx(
                     out=bank[:, i, :],
-                    lhsT=v[0][:].bitcast(FP8X4),
-                    lhsT_scale=v[1][:],
-                    rhs=w[0][:].bitcast(FP8X4),
-                    rhs_scale=w[1][:],
+                    lhsT=v_codes[:].bitcast(FP8X4),
+                    lhsT_scale=v_scales[:],
+                    rhs=w_codes[:].bitcast(FP8X4),
+                    rhs_scale=w_scales[:],
                     start=True,
                     stop=True,
                 )
-            y = keep.tile([P, len(blocks), HALF_Q], F32, name=name)
-            nc.scalar.copy(y[:], bank[:])
-            return [y[:, i, :] for i in range(len(blocks))]
+            sums = keep.tile([P, len(halves) * HALF_Q], F32, name=name)
+            nc.scalar.copy(sums[:], bank[:].rearrange("p h q -> p (h q)"))
+            return sums
 
-        def divisors():
+        def inverse_totals():
             nc.vector.reciprocal(inv_total[:], total[:])
-            bank = psum.tile([P, Q_BLOCKS, P], F32, name="bank")
-            for b in range(Q_BLOCKS):
+            bank = psum.tile([P, Q_CHUNKS, P], F32, name="bank")
+            for b in range(Q_CHUNKS):
                 nc.tensor.transpose(bank[:, b, :], inv_total[:, b : b + 1].to_broadcast([P, P]), ident[:])
-            spread = keep.tile([P, NQ], F32, name="spread")
-            nc.scalar.copy(spread[:], bank[:].rearrange("p b q -> p (b q)"))
-            return spread
+            inverse = keep.tile([P, NQ], F32, name="inverse")
+            nc.scalar.copy(inverse[:], bank[:].rearrange("p b q -> p (b q)"))
+            return inverse
 
-        def put_back(e, h, y, spread):
-            queries = slice(h * HALF_Q, (h + 1) * HALF_Q)
-            nc.vector.tensor_tensor(out_wins[e][:].indirect(lists[h]), y, spread[:, queries], MULT)
+        def put_back(e, listed, sums, inverse):
+            nc.vector.tensor_tensor(out_windows[e][:].indirect(listed), sums[:], inverse, MULT)
 
-        gather_last(0)
-        q0 = quantize_queries(0)
-        gather_last(1)
-        score0 = scores(0, *q0)
-        score1 = scores(1, *q0)
+        gather_last_queries(0)
+        q_half0 = quantize_queries(0)
+        gather_last_queries(1)
+        score0 = scores(0, *q_half0)
+        score1 = scores(1, *q_half0)
         prob0 = softmax(0, score0)
-        flat0 = weights_gpsimd(0, prob0)
-        q1 = quantize_queries(1)
+        weights0 = multiply_on_gpsimd(0, prob0)
+        q_half1 = quantize_queries(1)
         prob1 = softmax(1, score1)
-        flat1 = weights_gpsimd(1, prob1)
-        score2 = scores(2, *q1)
-        score3 = scores(3, *q1)
+        weights1 = multiply_on_gpsimd(1, prob1)
+        score2 = scores(2, *q_half1)
+        score3 = scores(3, *q_half1)
         prob2 = softmax(2, score2)
-        flat2 = weights_gpsimd(2, prob2)
+        weights2 = multiply_on_gpsimd(2, prob2)
         prob3 = softmax(3, score3)
-        turn_weights(0, flat0)
+        turn_weights(0, weights0)
         picked0 = gather_values(0)
-        v0_grouped = turn_values(0, picked0)
-        turned3 = turn(prob3)
-        turn_weights(1, flat1)
+        grouped0 = turn_values(0, picked0)
+        turned3 = turn_probs(prob3)
+        turn_weights(1, weights1)
         picked1 = gather_values(1)
-        v0 = quantize(v0_grouped[:], P, "v0")
-        w0 = quantize(w_grouped[0][:], HALF_Q, "w0")
-        spread = divisors()
-        turn_weights(2, flat2)
-        weights_vector(3, turned3)
-        v1_grouped = turn_values(1, picked1)
-        (y00,) = products([v0], w0, "y00")
-        w1 = quantize(w_grouped[1][:], HALF_Q, "w1")
-        v1 = quantize(v1_grouped[:], P, "v1")
-        y10, y11 = products([v0, v1], w1, "y1")
-        (y01,) = products([v1], w0, "y01")
-        put_back(0, 0, y00, spread)
-        put_back(0, 1, y10, spread)
-        nc.sync.dma_start(out[0:P, :], out_wins[0][:])
-        put_back(1, 0, y01, spread)
-        put_back(1, 1, y11, spread)
-        nc.sync.dma_start(out[P:DV, :], out_wins[1][:])
+        values0 = quantize(grouped0[:], P, "v0")
+        w_half0 = quantize(w_grouped[0][:], HALF_Q, "w0")
+        inverse = inverse_totals()
+        turn_weights(2, weights2)
+        multiply_on_vector(3, turned3)
+        grouped1 = turn_values(1, picked1)
+        sums00 = products(values0, [w_half0], "sums00")
+        w_half1 = quantize(w_grouped[1][:], HALF_Q, "w1")
+        values1 = quantize(grouped1[:], P, "v1")
+        sums01 = products(values0, [w_half1], "sums01")
+        sums1 = products(values1, [w_half0, w_half1], "sums1")
+
+        put_back(0, half_lists[0], sums00, inverse[:, half_queries[0]])
+        put_back(0, half_lists[1], sums01, inverse[:, half_queries[1]])
+        nc.sync.dma_start(out[0:P, :], out_windows[0][:])
+        put_back(1, q_list[:], sums1, inverse[:])
+        nc.sync.dma_start(out[P:DV, :], out_windows[1][:])

from contextlib import ExitStack

import concourse.mybir as mybir
from concourse.masks import make_identity

F32 = mybir.dt.float32
BF16 = mybir.dt.bfloat16
U32 = mybir.dt.uint32
U16 = mybir.dt.uint16
U8 = mybir.dt.uint8
FP8X4 = mybir.dt.float8_e4m3fn_x4
COPY_OUT = "p t x -> p x t"
EXP = mybir.ActivationFunctionType.Exp
MULT = mybir.AluOpType.mult
MAX = mybir.AluOpType.max
AXIS_X = mybir.AxisListType.X

P = 128
PACK = 4
T = 2048
D = 512
DV = 256
N = 512
NQ = 512
PER_LIST_COLUMN = 16
Q_CHUNKS = NQ // P
V_CHUNKS = DV // P
HALVES = 2
HALF_Q = NQ // HALVES
PSUM_BANKS = 8

FLOPS = 2 * NQ * N * D + 2 * NQ * N * DV
BYTES = 4 * (2 * D * T + DV * T + T + DV * T) + 2 * P * (N + NQ) // PER_LIST_COLUMN


def tile_attend_mod_sorted_kernel(tc, xq, kT, vT, vs, offs, qoffs, out):
    nc = tc.nc
    with ExitStack() as ctx:
        keep = ctx.enter_context(tc.tile_pool(name="keep", bufs=1))
        psum = ctx.enter_context(tc.psum_pool(name="psum", bufs=PSUM_BANKS))

        k_list = keep.tile([P, N // PER_LIST_COLUMN], U16, name="k_list")
        q_list = keep.tile([P, NQ // PER_LIST_COLUMN], U16, name="q_list")
        nc.sync.dma_start(k_list[:], offs)
        nc.sync.dma_start(q_list[:], qoffs)

        vs_window = keep.tile([P, T], F32, name="vs_window")
        nc.vector.memset(vs_window[:], 0.0)
        table_column = keep.tile([P, 1], F32, name="table_column")
        nc.vector.memset(table_column[:], 0.0)
        nc.scalar.activation(table_column[:], table_column[:], EXP)

        ident = keep.tile([P, P], F32, name="ident")
        make_identity(nc, ident[:])
        ident_bf16 = keep.tile([P, P], BF16, name="ident_bf16")
        nc.scalar.copy(ident_bf16[:], ident[:])
        out_windows = [keep.tile([P, T], F32, name="out_window%d" % e) for e in range(V_CHUNKS)]
        for window in out_windows:
            nc.gpsimd.memset(window[:], 0.0)

        def load(rows, name):
            tile = keep.tile([P, T], F32, name=name)
            nc.sync.dma_start(tile[:], rows)
            return tile

        k_rows = kT.rearrange("(p t) c -> p t c", t=PACK)
        q_rows = xq.rearrange("(p t) c -> p t c", t=PACK)
        k_tiles = [load(k_rows[:, 0, :], "k_tile0")]
        nc.sync.dma_start(vs_window[0:1, :], vs[0:1, :])
        k_tiles.extend([load(k_rows[:, t, :], "k_tile%d" % t) for t in range(1, PACK)])
        q_tiles = [load(q_rows[:, t, :], "q_tile%d" % t) for t in range(PACK)]
        v_tiles = [load(vT[e * P : (e + 1) * P, :], "v_tile%d" % e) for e in range(V_CHUNKS)]

        def quantize(grouped, width, name):
            codes = keep.tile([P, width], U32, align_bytes=64, name=name + "_codes")
            scales = keep.tile([P, width], U8, align_bytes=64, name=name + "_scales")
            nc.vector.quantize_mx(
                out=codes[:].bitcast(FP8X4),
                scales=scales[:],
                in_=grouped.rearrange("p c t -> p (c t)"),
            )
            return codes, scales

        k_grouped = keep.tile([P, N, PACK], BF16, align_bytes=64, name="k_grouped")
        nc.vector.tensor_copy(k_grouped[:, :, 0], k_tiles[0][:].indirect(k_list[:]))

        vs_picked = keep.tile([P, N], F32, name="vs_picked")
        nc.vector.tensor_copy(vs_picked[:], vs_window[:].indirect(k_list[:]))
        column_bank = psum.tile([P, PACK, P], F32, name="bank")
        for t in range(PACK):
            nc.tensor.transpose(column_bank[:, t, :], vs_picked[:, t::PACK], ident[:])
        vs_column = keep.tile([P, PACK], F32, name="vs_column")
        nc.scalar.copy(vs_column[:], column_bank[:, :, 0])
        row_bank = psum.tile([P, PACK, P], F32, name="bank")
        for t in range(PACK):
            nc.tensor.transpose(row_bank[:, t, :], vs_column[:, t : t + 1].to_broadcast([P, P]), ident[:])
        vs_row = keep.tile([P, PACK, P], F32, name="vs_row")
        nc.scalar.copy(vs_row[:], row_bank[:])

        for t in range(1, PACK):
            nc.vector.tensor_copy(k_grouped[:, :, t], k_tiles[t][:].indirect(k_list[:]))
        k_codes, k_scales = quantize(k_grouped[:], N, "k")

        q_grouped = keep.tile([P, NQ, PACK], BF16, align_bytes=64, name="q_grouped")
        for t in range(PACK - 1):
            nc.vector.tensor_copy(q_grouped[:, :, t], q_tiles[t][:].indirect(q_list[:]))

        half_queries = [slice(h * HALF_Q, (h + 1) * HALF_Q) for h in range(HALVES)]
        half_lists = [
            q_list[:, h * HALF_Q // PER_LIST_COLUMN : (h + 1) * HALF_Q // PER_LIST_COLUMN] for h in range(HALVES)
        ]
        neg_max = keep.tile([P, Q_CHUNKS], F32, name="neg_max")
        total = keep.tile([P, Q_CHUNKS], F32, name="total")
        inv_total = keep.tile([P, Q_CHUNKS], F32, name="inv_total")
        w_grouped = [keep.tile([P, HALF_Q, PACK], BF16, align_bytes=64, name="w_grouped%d" % h) for h in range(HALVES)]

        def gather_last_queries(h):
            last = PACK - 1
            nc.vector.tensor_copy(q_grouped[:, half_queries[h], last], q_tiles[last][:].indirect(half_lists[h]))

        def quantize_queries(h):
            return quantize(q_grouped[:, half_queries[h], :], HALF_Q, "q%d" % h)

        def scores(b, codes, scales):
            start = b * P % HALF_Q
            bank = psum.tile([P, N], F32, name="bank")
            nc.tensor.matmul_mx(
                out=bank[:],
                lhsT=codes[:, start : start + P].bitcast(FP8X4),
                lhsT_scale=scales[:, start : start + P],
                rhs=k_codes[:].bitcast(FP8X4),
                rhs_scale=k_scales[:],
                start=True,
                stop=True,
            )
            return bank

        def softmax(b, bank):
            nc.vector.tensor_reduce(neg_max[:, b : b + 1], bank[:], AXIS_X, MAX, negate=True)
            prob = keep.tile([P, PACK, P], F32, name="prob%d" % b)
            nc.scalar.activation(
                prob[:],
                bank[:].rearrange("p (s t) -> p t s", t=PACK),
                EXP,
                bias=neg_max[:, b : b + 1],
                accum_out=total[:, b : b + 1],
            )
            return prob

        def w_columns(b):
            h, i = divmod(b, Q_CHUNKS // HALVES)
            return w_grouped[h][:, i * P : (i + 1) * P, :]

        def multiply_on_gpsimd(b, prob):
            weights = keep.tile([P, PACK, P], BF16, name="weights%d" % b)
            nc.gpsimd.tensor_tensor(weights[:], prob[:], vs_row[:], MULT)
            return weights

        def turn_weights(b, weights):
            bank = psum.tile([P, PACK, P], BF16, name="bank")
            for t in range(PACK):
                nc.tensor.transpose(bank[:, t, :], weights[:, t, :], ident_bf16[:])
            nc.scalar.copy(w_columns(b), bank[:].rearrange(COPY_OUT))

        def turn_probs(prob):
            bank = psum.tile([P, PACK, P], F32, name="bank")
            for t in range(PACK):
                nc.tensor.transpose(bank[:, t, :], prob[:, t, :], ident[:])
            return bank

        def multiply_on_vector(b, bank):
            nc.vector.tensor_tensor(
                w_columns(b),
                bank[:].rearrange(COPY_OUT),
                vs_column[:].unsqueeze(1).to_broadcast([P, P, PACK]),
                MULT,
            )

        def gather_values(e):
            picked = keep.tile([P, N], F32, name="v_picked%d" % e)
            nc.vector.tensor_copy(picked[:], v_tiles[e][:].indirect(k_list[:]))
            return picked

        def turn_values(e, picked):
            bank = psum.tile([P, PACK, P], F32, name="bank")
            for t in range(PACK):
                nc.tensor.transpose(bank[:, t, :], picked[:, t::PACK], ident[:])
            grouped = keep.tile([P, P, PACK], BF16, align_bytes=64, name="v_grouped%d" % e)
            nc.scalar.copy(grouped[:], bank[:].rearrange(COPY_OUT))
            return grouped

        def products(values, halves, name):
            v_codes, v_scales = values
            bank = psum.tile([P, len(halves), HALF_Q], F32, name="bank")
            for i, (w_codes, w_scales) in enumerate(halves):
                nc.tensor.matmul_mx(
                    out=bank[:, i, :],
                    lhsT=v_codes[:].bitcast(FP8X4),
                    lhsT_scale=v_scales[:],
                    rhs=w_codes[:].bitcast(FP8X4),
                    rhs_scale=w_scales[:],
                    start=True,
                    stop=True,
                )
            sums = keep.tile([P, len(halves) * HALF_Q], F32, name=name)
            nc.scalar.copy(sums[:], bank[:].rearrange("p h q -> p (h q)"))
            return sums

        def inverse_totals():
            nc.vector.reciprocal(inv_total[:], total[:])
            bank = psum.tile([P, Q_CHUNKS, P], F32, name="bank")
            for b in range(Q_CHUNKS):
                nc.tensor.transpose(bank[:, b, :], inv_total[:, b : b + 1].to_broadcast([P, P]), ident[:])
            inverse = keep.tile([P, NQ], F32, name="inverse")
            nc.scalar.copy(inverse[:], bank[:].rearrange("p b q -> p (b q)"))
            return inverse

        def put_back(e, listed, sums, inverse):
            nc.vector.tensor_tensor(out_windows[e][:].indirect(listed), sums[:], inverse, MULT)

        gather_last_queries(0)
        q_half0 = quantize_queries(0)
        gather_last_queries(1)
        score0 = scores(0, *q_half0)
        score1 = scores(1, *q_half0)
        prob0 = softmax(0, score0)
        weights0 = multiply_on_gpsimd(0, prob0)
        q_half1 = quantize_queries(1)
        prob1 = softmax(1, score1)
        weights1 = multiply_on_gpsimd(1, prob1)
        score2 = scores(2, *q_half1)
        score3 = scores(3, *q_half1)
        prob2 = softmax(2, score2)
        weights2 = multiply_on_gpsimd(2, prob2)
        prob3 = softmax(3, score3)
        turn_weights(0, weights0)
        picked0 = gather_values(0)
        grouped0 = turn_values(0, picked0)
        turned3 = turn_probs(prob3)
        turn_weights(1, weights1)
        picked1 = gather_values(1)
        values0 = quantize(grouped0[:], P, "v0")
        w_half0 = quantize(w_grouped[0][:], HALF_Q, "w0")
        inverse = inverse_totals()
        turn_weights(2, weights2)
        multiply_on_vector(3, turned3)
        grouped1 = turn_values(1, picked1)
        sums00 = products(values0, [w_half0], "sums00")
        w_half1 = quantize(w_grouped[1][:], HALF_Q, "w1")
        values1 = quantize(grouped1[:], P, "v1")
        sums01 = products(values0, [w_half1], "sums01")
        sums1 = products(values1, [w_half0, w_half1], "sums1")

        put_back(0, half_lists[0], sums00, inverse[:, half_queries[0]])
        put_back(0, half_lists[1], sums01, inverse[:, half_queries[1]])
        nc.sync.dma_start(out[0:P, :], out_windows[0][:])
        put_back(1, q_list[:], sums1, inverse[:])
        nc.sync.dma_start(out[P:DV, :], out_windows[1][:])
